import numpy as np
import ml_dtypes


def mxq(x, axis, fmt="e4m3"):
    dtype, down = {"e4m3": (ml_dtypes.float8_e4m3fn, 7), "e5m2": (ml_dtypes.float8_e5m2, 14)}[fmt]
    v = np.moveaxis(np.asarray(x, np.float32).astype(ml_dtypes.bfloat16).astype(np.float64), axis, -1)
    blocks = v.reshape(v.shape[:-1] + (-1, 32))
    amax = np.abs(blocks).max(-1, keepdims=True)
    byte = np.maximum(np.where(amax > 0, np.frexp(amax)[1] - 1 + 127, 0) - down, 1)
    scale = np.exp2(byte - 127.0)
    codes = (blocks / scale).astype(np.float32).astype(dtype).astype(np.float64)
    return np.moveaxis((codes * scale).reshape(v.shape), -1, axis)


WIDE = False


def mx_kscale(k):
    if not WIDE:
        return np.ones(k)
    levels = np.array([10, -10, 5, -5, 0])
    if k % 512:
        return np.exp2(np.random.permutation(np.resize(levels, k // 32))).repeat(32)
    a = np.empty((k // 512, 16))
    for p in range(k // 512):
        a[p, :8] = np.random.permutation(np.resize(levels, 8))
        for g in range(8):
            far = levels[np.abs(levels - a[p, g]) >= 10]
            a[p, g + 8] = far[np.random.randint(len(far))]
    return np.exp2(a.ravel()).repeat(32)


def f64(x):
    return np.asarray(x).astype(np.float64)


def striped(idx):
    return np.tile(idx.reshape(-1, 16).T, (8, 1)).astype(np.uint16)


def unstriped(offs):
    return offs[:16].T.reshape(-1).astype(np.int64)


E2M1 = np.array([0.0, 0.5, 1.0, 1.5, 2.0, 3.0, 4.0, 6.0, -0.0, -0.5, -1.0, -1.5, -2.0, -3.0, -4.0, -6.0])


def pack_weight(w, fmt):
    k, n = w.shape
    w = f64(np.asarray(w, np.float32).astype(ml_dtypes.bfloat16)).reshape(k // 32, 32, n)
    amax = np.abs(w).max(1)
    if fmt == "e4m3":
        byte = np.frexp(amax)[1] - 1 + 127 - 7
    else:
        mant, ex = np.frexp(amax / 6.0)
        byte = np.where(mant > 0.5, ex, ex - 1) + 127
    byte = np.clip(np.where(amax > 0, byte, 1), 1, 254)
    scaled = (w * np.exp2(127.0 - byte)[:, None, :]).reshape(k, n).astype(np.float32)
    by_word = np.ascontiguousarray(scaled.reshape(k // 512, 128, 4, n).transpose(0, 1, 3, 2))
    if fmt == "e4m3":
        words = by_word.astype(ml_dtypes.float8_e4m3fn).view(np.uint8)
    else:
        c = by_word.astype(ml_dtypes.float4_e2m1fn).view(np.uint8) & 0xF
        words = (c[..., 0::2] | (c[..., 1::2] << 4)).reshape(k // 512, 128, 2 * n)
    return np.ascontiguousarray(words), np.ascontiguousarray(byte.astype(np.uint8).reshape(k // 512, 16, n))


def unpack_weight(words, scales, fmt):
    g, _, n = scales.shape
    words = np.ascontiguousarray(words).reshape(g, 128, n, -1)
    if fmt == "e4m3":
        vals = words.view(ml_dtypes.float8_e4m3fn).astype(np.float64)
    else:
        nib = np.empty((g, 128, n, 4), np.uint8)
        nib[..., 0::2] = words & 0xF
        nib[..., 1::2] = words >> 4
        vals = E2M1[nib]
    vals = vals * np.repeat(np.exp2(scales.astype(np.float64) - 127.0), 8, axis=1)[..., None]
    return vals.transpose(0, 1, 3, 2).reshape(g * 512, n)


def gelu(v):
    return 0.5 * v * (1.0 + np.tanh(np.sqrt(2.0 / np.pi) * (v + 0.044715 * v**3)))


def bf(x):
    return np.asarray(x, np.float32).astype(ml_dtypes.bfloat16)


def planes(Y):
    n, m = Y.shape
    b = f64(bf(Y)).reshape(n // 32, 32, m)
    amax = np.abs(b).max(1)
    byte = np.clip(np.where(amax > 0, np.frexp(amax)[1] - 1 + 127 - 7, 1), 1, 254)
    codes = (b * np.exp2(127.0 - byte)[:, None, :]).reshape(n, m).astype(np.float32).astype(ml_dtypes.float8_e4m3fn).view(np.uint8)
    words = codes.reshape(n // 512, 128, 4, m).transpose(0, 1, 3, 2)
    return np.ascontiguousarray(words), np.ascontiguousarray(byte.astype(np.uint8).reshape(n // 512, 16, m))


K, K2, H, N, T, S = 1024, 512, 1024, 512, 4096, 1024


def setup_inputs():
    n = np.random.standard_normal
    s = mx_kscale(K)[:, None]
    s2 = mx_kscale(K2)[:, None]
    u = mx_kscale(H)[:, None]
    d = {}
    d["tab_words"], d["tab_scales"] = pack_weight(n((K, T)) * s, "e4m3")
    d["offs"] = striped(np.random.permutation(T)[:S])
    d["xs_words"], d["xs_scales"] = pack_weight(n((K2, S)) * s2, "e4m3")
    d["w1"] = (0.7 * n((K, H)) / K ** 0.5 / s * u.T).astype(np.float32)
    d["wp"] = (1.3 * n((K2, H)) / K2 ** 0.5 / s2 * u.T).astype(np.float32)
    d["wq_words"], d["wq_scales"] = pack_weight(1.3 * n((K2, H)) / K2 ** 0.5 / s2, "e2m1")
    w4 = n((H, N)) / H ** 0.5 / u * np.exp(0.8 * n(N))
    d["w4_words"], d["w4_scales"] = pack_weight(w4, "e4m3")
    d["place"] = n((N, S)).astype(np.float32)
    return d


def reference(tab_words, tab_scales, offs, xs_words, xs_scales, w1, wp,
              wq_words, wq_scales, w4_words, w4_scales, place):
    v = unpack_weight(tab_words, tab_scales, "e4m3")[:, unstriped(offs)]
    xs = unpack_weight(xs_words, xs_scales, "e4m3")
    wq = unpack_weight(wq_words, wq_scales, "e2m1")
    w4 = unpack_weight(w4_words, w4_scales, "e4m3")
    dev = mxq(f64(wp), 0, "e4m3").T @ xs
    rough = wq.T @ xs
    blank = mxq(f64(w1), 0, "e4m3").T @ v
    h = dev / (1.0 + np.square(rough)) + blank
    y = (w4.T @ mxq(h, 0, "e4m3")) * f64(place)
    words, scales = planes(y)
    return y, words, scales

@@ -1,0 +1,284 @@
+from contextlib import ExitStack
+
+import concourse.mybir as mybir
+
+K, K2, H, N, T, S = 1024, 512, 1024, 512, 4096, 1024
+FLOPS = 2 * S * (K * H + 2 * K2 * H + H * N)
+
+F32 = mybir.dt.float32
+BF16 = mybir.dt.bfloat16
+I32 = mybir.dt.int32
+U32 = mybir.dt.uint32
+U16 = mybir.dt.uint16
+U8 = mybir.dt.uint8
+FP8X4 = mybir.dt.float8_e4m3fn_x4
+FP4X4 = mybir.dt.float4_e2m1fn_x4
+ACT = mybir.ActivationFunctionType
+ALU = mybir.AluOpType
+
+P = 128
+PACK = 4
+PASS = P * PACK
+COLS = 128
+CHUNKS = S // COLS
+PAIR = 2 * COLS
+
+
+def tile_list_lens_path_correction_kernel(
+    tc, tab_words, tab_scales, offs, xs_words, xs_scales, w1, wp,
+    wq_words, wq_scales, w4_words, w4_scales, place, out_0, out_1, out_2,
+):
+    nc = tc.nc
+    with ExitStack() as ctx:
+        keep = ctx.enter_context(tc.tile_pool(name="keep", bufs=1))
+        ring = ctx.enter_context(tc.tile_pool(name="ring", bufs=3))
+        psum = ctx.enter_context(tc.psum_pool(name="psum", bufs=2))
+
+        def held(shape, dtype, name, over=None):
+            return keep.tile(shape, dtype, name=name, tag=over or name, align_bytes=64)
+
+        def load_words(tile, words):
+            nc.sync.dma_start(out=tile[:].bitcast(I32), in_=words.bitcast(I32))
+
+        def load_scale_rows(queue, tile, scales):
+            passes = scales.shape[0]
+            for quad in range(4):
+                rows = scales[:, 4 * quad : 4 * quad + 4, :].bitcast(I32)
+                queue.dma_start(out=tile[32 * quad : 32 * quad + 4 * passes, :].bitcast(I32), in_=rows)
+
+        offsets = keep.tile([P, S // 16], U16, name="offsets")
+        wq_raw = held([P, H], U16, "wq_raw")
+        wq_raw_scales = held([P, H], U8, "wq_raw_scales")
+        xs_codes = held([P, S], U32, "xs_codes")
+        xs_plane = held([P, S], U8, "xs_plane")
+        tab_plane = held([P, T], U8, "tab_plane")
+        w4_raw_scales = held([P, N], U8, "w4_raw_scales")
+        tab_codes = [held([P, T], U32, f"tab_codes{a}") for a in range(2)]
+        w4_raw = held([P, 2, N], I32, "w4_raw")
+        place_sb = [held([P, PACK, S // 2], F32, f"place{half}") for half in range(2)]
+
+        for plane in (wq_raw_scales, xs_plane):
+            nc.gpsimd.memset(plane[:].bitcast(I32), 0)
+        for plane in (tab_plane, w4_raw_scales):
+            nc.vector.memset(plane[:].bitcast(I32), 0)
+
+        def load_weight(w, a, b, name):
+            raw = held([P, PACK, PASS], F32, name)
+            rows = w[a * PASS : (a + 1) * PASS, b * PASS : (b + 1) * PASS]
+            nc.sync.dma_start(out=raw[:], in_=rows.rearrange("(p i) c -> p i c", i=PACK))
+            return raw
+
+        wp_raw = [load_weight(wp, 0, 0, "wp_raw0")]
+        load_words(wq_raw, wq_words[0])
+        load_scale_rows(nc.sync, wq_raw_scales, wq_scales)
+        load_words(xs_codes, xs_words[0].rearrange("p c i -> p (c i)"))
+        load_scale_rows(nc.sync, xs_plane, xs_scales)
+        w1_raw = {(0, 0): load_weight(w1, 0, 0, "w1_raw00")}
+        load_scale_rows(nc.sync, tab_plane, tab_scales)
+        nc.sync.dma_start(offsets[:], offs)
+        w1_raw[1, 0] = load_weight(w1, 1, 0, "w1_raw10")
+        load_scale_rows(nc.sync, w4_raw_scales, w4_scales)
+        for a in range(2):
+            load_words(tab_codes[a], tab_words[a].rearrange("p c i -> p (c i)"))
+        wp_raw.append(load_weight(wp, 0, 1, "wp_raw1"))
+        for a in range(2):
+            w1_raw[a, 1] = load_weight(w1, a, 1, f"w1_raw{a}1")
+        nc.sync.dma_start(out=w4_raw[:], in_=w4_words.rearrange("a p c i -> p a (c i)").bitcast(I32))
+        for half in range(2):
+            cols = slice(half * S // 2, (half + 1) * S // 2)
+            nc.sync.dma_start(out=place_sb[half][:], in_=place[:, cols].rearrange("(p t) j -> p t j", t=PACK))
+
+        wq_codes = held([P, H], U16, "wq_codes")
+        wq_plane = held([P, H], U8, "wq_plane")
+        for b in range(2):
+            cols = slice(b * PASS, (b + 1) * PASS)
+            for dealt, natural in ((wq_codes, wq_raw), (wq_plane, wq_raw_scales)):
+                nc.vector.tensor_copy(
+                    out=dealt[:, cols].rearrange("p (t m) -> p t m", t=PACK),
+                    in_=natural[:, cols].rearrange("p (m t) -> p t m", t=PACK),
+                )
+
+        def round_weight(engine, raw, name, over=None):
+            rounded = held([P, PASS * PACK], BF16, name, over)
+            dst = rounded[:].rearrange("p (t m i) -> p m i t", t=PACK, i=PACK)
+            src = raw[:].rearrange("p i (m t) -> p m i t", t=PACK)
+            if engine is nc.vector:
+                nc.vector.tensor_copy(out=dst, in_=src)
+            else:
+                nc.scalar.copy(out=dst, in_=src)
+            return rounded
+
+        def quantise(rounded, name, over=None):
+            width = rounded.shape[1] // PACK
+            codes = held([P, width], U32, name + "_codes", over)
+            plane = held([P, width], U8, name + "_plane")
+            nc.vector.quantize_mx(out=codes[:].bitcast(FP8X4), scales=plane[:], in_=rounded[:])
+            return codes, plane
+
+        def product(name, passes, chunk):
+            bank = psum.tile([P, PACK, COLS], F32, name=name)
+            cols = slice(chunk * COLS, (chunk + 1) * COLS)
+            for t in range(PACK):
+                rows = slice(t * P, (t + 1) * P)
+                for n, (w_codes, w_plane, x_codes, x_plane, w_dtype) in enumerate(passes):
+                    nc.tensor.matmul_mx(
+                        out=bank[:, t, :],
+                        lhsT=w_codes[:, rows].bitcast(w_dtype),
+                        lhsT_scale=w_plane[:, rows],
+                        rhs=x_codes[:, cols].bitcast(FP8X4),
+                        rhs_scale=x_plane[:, cols],
+                        start=(n == 0),
+                        stop=(n == len(passes) - 1),
+                    )
+            return bank
+
+        def woven(bank):
+            return bank[:].rearrange("p t c -> p c t")
+
+        def as_woven(ap):
+            return ap.rearrange("p (c t) -> p c t", t=PACK)
+
+        factors = {}
+        terms = {}
+
+        def damping(b, pair, squares, roots):
+            cols = slice(b * PASS, (b + 1) * PASS)
+            square = squares[:, pair % 2, :]
+            root = roots[:, pair % 2, :]
+            for half in range(2):
+                bank = product("rough", [(wq_codes[:, cols], wq_plane[:, cols], xs_codes[:], xs_plane[:], FP4X4)], 2 * pair + half)
+                nc.scalar.activation(out=as_woven(square[:, half * PASS : (half + 1) * PASS]), in_=woven(bank), func=ACT.Square)
+            nc.scalar.activation(out=root, in_=square, func=ACT.Abs_reciprocal_sqrt, bias=1.0)
+            factor = held([P, 2 * PASS], F32, f"factor{b}_{pair}")
+            nc.scalar.activation(out=factor[:], in_=root, func=ACT.Square)
+            factors[b, pair] = factor
+
+        def damped_dev(b, pair, wp_mx, term):
+            for half in range(2):
+                bank = product("dev", [(wp_mx[0][:], wp_mx[1][:], xs_codes[:], xs_plane[:], FP8X4)], 2 * pair + half)
+                cols = slice(half * PASS, (half + 1) * PASS)
+                nc.vector.tensor_tensor(
+                    out=as_woven(term[:, cols]), in0=woven(bank), in1=as_woven(factors[b, pair][:, cols]), op=ALU.mult
+                )
+            terms[b, pair] = term
+
+        v_codes = [held([P, S], U32, f"v_codes{a}") for a in range(2)]
+        v_plane = held([P, S], U8, "v_plane")
+
+        def add_blank(b, chunk, w1_mx, h_round):
+            passes = [(w1_mx[a][0][:], w1_mx[a][1][:], v_codes[a][:], v_plane[4 * a :, :], FP8X4) for a in range(2)]
+            bank = product("blank", passes, chunk)
+            term = terms[b, chunk // 2][:, chunk % 2 * PASS : (chunk % 2 + 1) * PASS]
+            nc.vector.tensor_tensor(out=as_woven(h_round), in0=woven(bank), in1=as_woven(term), op=ALU.add)
+
+        h_codes = [held([P, S], U32, f"h_codes{b}") for b in range(2)]
+        h_plane = [held([P, S], U8, f"h_plane{b}") for b in range(2)]
+
+        def quantise_h(b, pair, h_round):
+            cols = slice(pair * PAIR, (pair + 1) * PAIR)
+            nc.vector.quantize_mx(out=h_codes[b][:, cols].bitcast(FP8X4), scales=h_plane[b][:, cols], in_=h_round[:])
+
+        pairs = CHUNKS // 2
+        squares = held([P, 2, 2 * PASS], F32, "squares0")
+        roots = held([P, 2, 2 * PASS], F32, "roots0")
+        wp_mx0 = quantise(round_weight(nc.scalar, wp_raw[0], "wp_round0"), "wp0")
+        for pair in range(pairs):
+            damping(0, pair, squares, roots)
+        w1_round = [round_weight(nc.vector, w1_raw[a, 0], f"w1_round{a}0") for a in range(2)]
+        w1_mx0 = [quantise(w1_round[a], f"w1_{a}0") for a in range(2)]
+        w4_plane = held([P, N], U8, "w4_plane")
+        nc.vector.tensor_copy(
+            out=w4_plane[:].rearrange("p (t m) -> p t m", t=PACK),
+            in_=w4_raw_scales[:].rearrange("p (m t) -> p t m", t=PACK),
+        )
+        nc.vector.tensor_copy(v_plane[:], tab_plane[:].indirect(offsets[:]))
+        for a in range(2):
+            nc.vector.tensor_copy(v_codes[a][:], tab_codes[a][:].indirect(offsets[:]))
+        spent = ["w1_raw00", "w1_raw10", "tab_codes0", "tab_codes1"]
+        for pair in range(pairs):
+            damped_dev(0, pair, wp_mx0, held([P, 2 * PASS], F32, f"term{pair}", spent[pair]))
+
+        wp_round1 = round_weight(nc.scalar, wp_raw[1], "wp_round1", "squares0")
+        w1_round01 = round_weight(nc.scalar, w1_raw[0, 1], "w1_round01", "roots0")
+        squares = held([P, 2, 2 * PASS], F32, "squares1", "w1_raw01")
+        roots = held([P, 2, 2 * PASS], F32, "roots1", "wp_raw1")
+        damping(1, 0, squares, roots)
+
+        previous = None
+        for pair in range(pairs):
+            h_round = ring.tile([P, 2 * PASS], BF16, name="h_round", align_bytes=64)
+            add_blank(0, 2 * pair, w1_mx0, h_round[:, :PASS])
+            if previous is not None:
+                quantise_h(0, pair - 1, previous)
+            add_blank(0, 2 * pair + 1, w1_mx0, h_round[:, PASS:])
+            previous = h_round
+        wp_mx1 = quantise(wp_round1, "wp1", spent[0])
+        w1_mx1 = [quantise(w1_round01, "w1_01", spent[1])]
+        w1_round11 = round_weight(nc.vector, w1_raw[1, 1], "w1_round11", spent[3])
+        w4_codes = held([P, 2, N], I32, "w4_codes", spent[2])
+        nc.vector.tensor_copy(
+            out=w4_codes[:].rearrange("p a (t g m) -> p a g t m", t=PACK, m=4),
+            in_=w4_raw[:].rearrange("p a (g m t) -> p a g t m", t=PACK, m=4),
+        )
+        w1_mx1.append(quantise(w1_round11, "w1_11"))
+        quantise_h(0, pairs - 1, previous)
+
+        y_codes = held([P, S], U32, "y_codes")
+        y_plane = held([P, S], U8, "y_plane")
+        y_sb = [held([P, PACK, PAIR], F32, f"y{pair}", f"factor0_{pair}") for pair in range(CHUNKS // 2)]
+        h_rounds = {}
+        y_rounds = {}
+
+        def second_rows(pair):
+            h_round = ring.tile([P, 2 * PASS], BF16, name="h_round", align_bytes=64)
+            damped_dev(1, pair, wp_mx1, factors[1, pair])
+            for half in range(2):
+                add_blank(1, 2 * pair + half, w1_mx1, h_round[:, half * PASS : (half + 1) * PASS])
+            h_rounds[pair] = h_round
+
+        def weigh(pair):
+            passes = [(w4_codes[:, a, :], w4_plane[4 * a :, :], h_codes[a][:], h_plane[a][:], FP8X4) for a in range(2)]
+            for half in range(2):
+                chunk = 2 * pair + half
+                bank = product("mixed", passes, chunk)
+                first = chunk * COLS % (S // 2)
+                nc.vector.tensor_tensor(
+                    out=y_sb[pair][:, :, half * COLS : (half + 1) * COLS],
+                    in0=bank[:],
+                    in1=place_sb[pair // 2][:, :, first : first + COLS],
+                    op=ALU.mult,
+                )
+            cols = slice(pair * PAIR, (pair + 1) * PAIR)
+            nc.sync.dma_start(out=out_0[:, cols].rearrange("(p t) j -> p t j", t=PACK), in_=y_sb[pair][:])
+            y_round = ring.tile([P, PAIR * PACK], BF16, name="y_round", align_bytes=64)
+            nc.scalar.copy(
+                out=y_round[:].rearrange("p (g c t) -> p g t c", t=PACK, c=4),
+                in_=y_sb[pair][:].rearrange("p t (g c) -> p g t c", c=4),
+            )
+            y_rounds[pair] = y_round
+
+        def quantise_y(pair):
+            cols = slice(pair * PAIR, (pair + 1) * PAIR)
+            nc.vector.quantize_mx(out=y_codes[:, cols].bitcast(FP8X4), scales=y_plane[:, cols], in_=y_rounds[pair][:])
+            nc.sync.dma_start(
+                out=out_1[0].rearrange("p c i -> p (c i)").bitcast(I32)[:, cols],
+                in_=y_codes[:, cols].bitcast(I32),
+            )
+
+        for step in range(pairs + 2):
+            if step + 1 < pairs:
+                damping(1, step + 1, squares, roots)
+            if step < pairs:
+                second_rows(step)
+            if 1 <= step <= pairs:
+                weigh(step - 1)
+            if step < pairs:
+                quantise_h(1, step, h_rounds[step])
+            if step >= 2:
+                quantise_y(step - 2)
+        for quad in range(4):
+            queue = nc.sync if quad % 2 == 0 else nc.scalar
+            queue.dma_start(
+                out=out_2[0, 4 * quad : 4 * quad + 4, :].bitcast(I32),
+                in_=y_plane[32 * quad : 32 * quad + 4, :].bitcast(I32),
+            )

@@ -32,7 +32,7 @@ def tile_list_lens_path_correction_kernel(
     with ExitStack() as ctx:
         keep = ctx.enter_context(tc.tile_pool(name="keep", bufs=1))
         ring = ctx.enter_context(tc.tile_pool(name="ring", bufs=3))
-        psum = ctx.enter_context(tc.psum_pool(name="psum", bufs=2))
+        psum = ctx.enter_context(tc.psum_pool(name="psum", bufs=1))
 
         def held(shape, dtype, name, over=None):
             return keep.tile(shape, dtype, name=name, tag=over or name, align_bytes=64)
@@ -68,18 +68,18 @@ def tile_list_lens_path_correction_kernel(
             nc.sync.dma_start(out=raw[:], in_=rows.rearrange("(p i) c -> p i c", i=PACK))
             return raw
 
-        wp_raw = [load_weight(wp, 0, 0, "wp_raw0")]
+        load_words(xs_codes, xs_words[0].rearrange("p c i -> p (c i)"))
         load_words(wq_raw, wq_words[0])
         load_scale_rows(nc.sync, wq_raw_scales, wq_scales)
-        load_words(xs_codes, xs_words[0].rearrange("p c i -> p (c i)"))
         load_scale_rows(nc.sync, xs_plane, xs_scales)
-        w1_raw = {(0, 0): load_weight(w1, 0, 0, "w1_raw00")}
         load_scale_rows(nc.sync, tab_plane, tab_scales)
         nc.sync.dma_start(offsets[:], offs)
+        wp_raw = [load_weight(wp, 0, 0, "wp_raw0")]
+        w1_raw = {(0, 0): load_weight(w1, 0, 0, "w1_raw00")}
+        load_words(tab_codes[0], tab_words[0].rearrange("p c i -> p (c i)"))
         w1_raw[1, 0] = load_weight(w1, 1, 0, "w1_raw10")
         load_scale_rows(nc.sync, w4_raw_scales, w4_scales)
-        for a in range(2):
-            load_words(tab_codes[a], tab_words[a].rearrange("p c i -> p (c i)"))
+        load_words(tab_codes[1], tab_words[1].rearrange("p c i -> p (c i)"))
         wp_raw.append(load_weight(wp, 0, 1, "wp_raw1"))
         for a in range(2):
             w1_raw[a, 1] = load_weight(w1, a, 1, f"w1_raw{a}1")
@@ -115,14 +115,14 @@ def tile_list_lens_path_correction_kernel(
             nc.vector.quantize_mx(out=codes[:].bitcast(FP8X4), scales=plane[:], in_=rounded[:])
             return codes, plane
 
-        def product(name, passes, chunk):
-            bank = psum.tile([P, PACK, COLS], F32, name=name)
-            cols = slice(chunk * COLS, (chunk + 1) * COLS)
-            for t in range(PACK):
+        def product(bank_number, passes, slices, cols):
+            width = cols.stop - cols.start
+            bank = psum.tile([P, len(slices), width], F32, name=f"bank{bank_number}")
+            for place_in_bank, t in enumerate(slices):
                 rows = slice(t * P, (t + 1) * P)
                 for n, (w_codes, w_plane, x_codes, x_plane, w_dtype) in enumerate(passes):
                     nc.tensor.matmul_mx(
-                        out=bank[:, t, :],
+                        out=bank[:, place_in_bank, :],
                         lhsT=w_codes[:, rows].bitcast(w_dtype),
                         lhsT_scale=w_plane[:, rows],
                         rhs=x_codes[:, cols].bitcast(FP8X4),
@@ -131,6 +131,16 @@ def tile_list_lens_path_correction_kernel(
                         stop=(n == len(passes) - 1),
                     )
             return bank
+
+        def chunk_cols(chunk):
+            return slice(chunk * COLS, (chunk + 1) * COLS)
+
+        taken = []
+
+        def next_banks():
+            first_bank = 2 * len(taken) % 8
+            taken.append(first_bank)
+            return first_bank
 
         def woven(bank):
             return bank[:].rearrange("p t c -> p c t")
@@ -141,120 +151,136 @@ def tile_list_lens_path_correction_kernel(
         factors = {}
         terms = {}
 
-        def damping(b, pair, squares, roots):
+        def square_rough(b, pair):
             cols = slice(b * PASS, (b + 1) * PASS)
-            square = squares[:, pair % 2, :]
-            root = roots[:, pair % 2, :]
-            for half in range(2):
-                bank = product("rough", [(wq_codes[:, cols], wq_plane[:, cols], xs_codes[:], xs_plane[:], FP4X4)], 2 * pair + half)
-                nc.scalar.activation(out=as_woven(square[:, half * PASS : (half + 1) * PASS]), in_=woven(bank), func=ACT.Square)
-            nc.scalar.activation(out=root, in_=square, func=ACT.Abs_reciprocal_sqrt, bias=1.0)
+            passes = [(wq_codes[:, cols], wq_plane[:, cols], xs_codes[:], xs_plane[:], FP4X4)]
             factor = held([P, 2 * PASS], F32, f"factor{b}_{pair}")
-            nc.scalar.activation(out=factor[:], in_=root, func=ACT.Square)
+            first_bank = next_banks()
+            for half in range(2):
+                bank = product(first_bank + half, passes, range(PACK), chunk_cols(2 * pair + half))
+                nc.scalar.activation(out=as_woven(factor[:, half * PASS : (half + 1) * PASS]), in_=woven(bank), func=ACT.Square)
             factors[b, pair] = factor
 
+        def damping(b, pair, roots):
+            root = roots[:, pair % 2, :]
+            nc.scalar.activation(out=root, in_=factors[b, pair][:], func=ACT.Abs_reciprocal_sqrt, bias=1.0)
+            nc.scalar.activation(out=factors[b, pair][:], in_=root, func=ACT.Square)
+
         def damped_dev(b, pair, wp_mx, term):
+            first_bank = next_banks()
             for half in range(2):
-                bank = product("dev", [(wp_mx[0][:], wp_mx[1][:], xs_codes[:], xs_plane[:], FP8X4)], 2 * pair + half)
+                passes = [(wp_mx[0][:], wp_mx[1][:], xs_codes[:], xs_plane[:], FP8X4)]
+                bank = product(first_bank + half, passes, range(PACK), chunk_cols(2 * pair + half))
                 cols = slice(half * PASS, (half + 1) * PASS)
                 nc.vector.tensor_tensor(
                     out=as_woven(term[:, cols]), in0=woven(bank), in1=as_woven(factors[b, pair][:, cols]), op=ALU.mult
                 )
             terms[b, pair] = term
 
-        v_codes = [held([P, S], U32, f"v_codes{a}") for a in range(2)]
+        v_codes = []
         v_plane = held([P, S], U8, "v_plane")
 
-        def add_blank(b, chunk, w1_mx, h_round):
+        h_rounds = {}
+
+        def add_blank(b, pair, w1_mx):
             passes = [(w1_mx[a][0][:], w1_mx[a][1][:], v_codes[a][:], v_plane[4 * a :, :], FP8X4) for a in range(2)]
-            bank = product("blank", passes, chunk)
-            term = terms[b, chunk // 2][:, chunk % 2 * PASS : (chunk % 2 + 1) * PASS]
-            nc.vector.tensor_tensor(out=as_woven(h_round), in0=woven(bank), in1=as_woven(term), op=ALU.add)
+            h_round = ring.tile([P, 2 * PASS], BF16, name="h_round", align_bytes=64)
+            first_bank = next_banks()
+            for half in range(2):
+                bank = product(first_bank + half, passes, range(PACK), chunk_cols(2 * pair + half))
+                cols = slice(half * PASS, (half + 1) * PASS)
+                nc.vector.tensor_tensor(
+                    out=as_woven(h_round[:, cols]), in0=woven(bank), in1=as_woven(terms[b, pair][:, cols]), op=ALU.add
+                )
+            h_rounds[b, pair] = h_round
 
         h_codes = [held([P, S], U32, f"h_codes{b}") for b in range(2)]
         h_plane = [held([P, S], U8, f"h_plane{b}") for b in range(2)]
 
-        def quantise_h(b, pair, h_round):
+        def quantise_h(b, pair):
             cols = slice(pair * PAIR, (pair + 1) * PAIR)
-            nc.vector.quantize_mx(out=h_codes[b][:, cols].bitcast(FP8X4), scales=h_plane[b][:, cols], in_=h_round[:])
+            nc.vector.quantize_mx(out=h_codes[b][:, cols].bitcast(FP8X4), scales=h_plane[b][:, cols], in_=h_rounds[b, pair][:])
 
         pairs = CHUNKS // 2
-        squares = held([P, 2, 2 * PASS], F32, "squares0")
+        for b in range(2):
+            for pair in range(pairs):
+                square_rough(b, pair)
         roots = held([P, 2, 2 * PASS], F32, "roots0")
-        wp_mx0 = quantise(round_weight(nc.scalar, wp_raw[0], "wp_round0"), "wp0")
         for pair in range(pairs):
-            damping(0, pair, squares, roots)
-        w1_round = [round_weight(nc.vector, w1_raw[a, 0], f"w1_round{a}0") for a in range(2)]
-        w1_mx0 = [quantise(w1_round[a], f"w1_{a}0") for a in range(2)]
+            damping(0, pair, roots)
+
+        def gather_words(a, pieces):
+            v_codes.append(held([P, S], U32, f"v_codes{a}"))
+            width = S // pieces
+            for first in range(0, S, width):
+                picks = offsets[:, first // 16 : (first + width) // 16]
+                nc.vector.tensor_copy(v_codes[a][:, first : first + width], tab_codes[a][:].indirect(picks))
+
+        nc.vector.tensor_copy(v_plane[:], tab_plane[:].indirect(offsets[:]))
+        wp_round0 = round_weight(nc.vector, wp_raw[0], "wp_round0")
+        w1_round00 = round_weight(nc.vector, w1_raw[0, 0], "w1_round00")
+        wp_mx0 = quantise(wp_round0, "wp0")
+        w1_mx0 = [quantise(w1_round00, "w1_00")]
+        gather_words(0, 1)
+        w1_round10 = round_weight(nc.vector, w1_raw[1, 0], "w1_round10")
         w4_plane = held([P, N], U8, "w4_plane")
         nc.vector.tensor_copy(
             out=w4_plane[:].rearrange("p (t m) -> p t m", t=PACK),
             in_=w4_raw_scales[:].rearrange("p (m t) -> p t m", t=PACK),
         )
-        nc.vector.tensor_copy(v_plane[:], tab_plane[:].indirect(offsets[:]))
-        for a in range(2):
-            nc.vector.tensor_copy(v_codes[a][:], tab_codes[a][:].indirect(offsets[:]))
-        spent = ["w1_raw00", "w1_raw10", "tab_codes0", "tab_codes1"]
-        for pair in range(pairs):
-            damped_dev(0, pair, wp_mx0, held([P, 2 * PASS], F32, f"term{pair}", spent[pair]))
+        w1_mx0.append(quantise(w1_round10, "w1_10"))
+        early_terms = held([P, 2, 2 * PASS], F32, "early_terms", "w1_raw10")
+        for pair in range(2):
+            damped_dev(0, pair, wp_mx0, early_terms[:, pair, :])
+        gather_words(1, 2)
+        late_terms = held([P, 2, 2 * PASS], F32, "late_terms", "tab_codes1")
+        wp_round1 = round_weight(nc.scalar, wp_raw[1], "wp_round1", "roots0")
+        w1_round01 = round_weight(nc.scalar, w1_raw[0, 1], "w1_round01", "wp_raw1")
+        w1_round11 = round_weight(nc.scalar, w1_raw[1, 1], "w1_round11", "w1_raw01")
+        roots = held([P, 2, 2 * PASS], F32, "roots1", "w1_raw11")
+        damping(1, 0, roots)
 
-        wp_round1 = round_weight(nc.scalar, wp_raw[1], "wp_round1", "squares0")
-        w1_round01 = round_weight(nc.scalar, w1_raw[0, 1], "w1_round01", "roots0")
-        squares = held([P, 2, 2 * PASS], F32, "squares1", "w1_raw01")
-        roots = held([P, 2, 2 * PASS], F32, "roots1", "wp_raw1")
-        damping(1, 0, squares, roots)
-
-        previous = None
         for pair in range(pairs):
-            h_round = ring.tile([P, 2 * PASS], BF16, name="h_round", align_bytes=64)
-            add_blank(0, 2 * pair, w1_mx0, h_round[:, :PASS])
-            if previous is not None:
-                quantise_h(0, pair - 1, previous)
-            add_blank(0, 2 * pair + 1, w1_mx0, h_round[:, PASS:])
-            previous = h_round
-        wp_mx1 = quantise(wp_round1, "wp1", spent[0])
-        w1_mx1 = [quantise(w1_round01, "w1_01", spent[1])]
-        w1_round11 = round_weight(nc.vector, w1_raw[1, 1], "w1_round11", spent[3])
-        w4_codes = held([P, 2, N], I32, "w4_codes", spent[2])
+            if 1 <= pair < pairs - 1:
+                damped_dev(0, pair + 1, wp_mx0, late_terms[:, pair - 1, :])
+            add_blank(0, pair, w1_mx0)
+            if pair >= 1:
+                quantise_h(0, pair - 1)
+        wp_mx1 = quantise(wp_round1, "wp1")
+        quantise_h(0, pairs - 1)
+        w1_mx1 = [quantise(w1_round01, "w1_01")]
+        w4_codes = held([P, 2, N], I32, "w4_codes", "tab_codes1")
         nc.vector.tensor_copy(
             out=w4_codes[:].rearrange("p a (t g m) -> p a g t m", t=PACK, m=4),
             in_=w4_raw[:].rearrange("p a (g m t) -> p a g t m", t=PACK, m=4),
         )
         w1_mx1.append(quantise(w1_round11, "w1_11"))
-        quantise_h(0, pairs - 1, previous)
 
         y_codes = held([P, S], U32, "y_codes")
         y_plane = held([P, S], U8, "y_plane")
         y_sb = [held([P, PACK, PAIR], F32, f"y{pair}", f"factor0_{pair}") for pair in range(CHUNKS // 2)]
-        h_rounds = {}
         y_rounds = {}
-
-        def second_rows(pair):
-            h_round = ring.tile([P, 2 * PASS], BF16, name="h_round", align_bytes=64)
-            damped_dev(1, pair, wp_mx1, factors[1, pair])
-            for half in range(2):
-                add_blank(1, 2 * pair + half, w1_mx1, h_round[:, half * PASS : (half + 1) * PASS])
-            h_rounds[pair] = h_round
 
         def weigh(pair):
             passes = [(w4_codes[:, a, :], w4_plane[4 * a :, :], h_codes[a][:], h_plane[a][:], FP8X4) for a in range(2)]
+            y_round = ring.tile([P, PAIR * PACK], BF16, name="y_round", align_bytes=64)
+            first_bank = next_banks()
             for half in range(2):
                 chunk = 2 * pair + half
-                bank = product("mixed", passes, chunk)
+                bank = product(first_bank + half, passes, range(PACK), chunk_cols(chunk))
                 first = chunk * COLS % (S // 2)
+                y = y_sb[pair][:, :, chunk_cols(half)]
                 nc.vector.tensor_tensor(
-                    out=y_sb[pair][:, :, half * COLS : (half + 1) * COLS],
-                    in0=bank[:],
-                    in1=place_sb[pair // 2][:, :, first : first + COLS],
-                    op=ALU.mult,
+                    out=y, in0=bank[:], in1=place_sb[pair // 2][:, :, first : first + COLS], op=ALU.mult
                 )
+                dst = y_round[:, half * PASS : (half + 1) * PASS].rearrange("p (g c t) -> p g t c", t=PACK, c=4)
+                src = y.rearrange("p t (g c) -> p g t c", c=4)
+                if chunk == CHUNKS - 1:
+                    nc.vector.tensor_copy(out=dst, in_=src)
+                else:
+                    nc.scalar.copy(out=dst, in_=src)
             cols = slice(pair * PAIR, (pair + 1) * PAIR)
             nc.sync.dma_start(out=out_0[:, cols].rearrange("(p t) j -> p t j", t=PACK), in_=y_sb[pair][:])
-            y_round = ring.tile([P, PAIR * PACK], BF16, name="y_round", align_bytes=64)
-            nc.scalar.copy(
-                out=y_round[:].rearrange("p (g c t) -> p g t c", t=PACK, c=4),
-                in_=y_sb[pair][:].rearrange("p t (g c) -> p g t c", c=4),
-            )
             y_rounds[pair] = y_round
 
         def quantise_y(pair):
@@ -267,15 +293,16 @@ def tile_list_lens_path_correction_kernel(
 
         for step in range(pairs + 2):
             if step + 1 < pairs:
-                damping(1, step + 1, squares, roots)
+                damping(1, step + 1, roots)
             if step < pairs:
-                second_rows(step)
-            if 1 <= step <= pairs:
-                weigh(step - 1)
-            if step < pairs:
-                quantise_h(1, step, h_rounds[step])
+                damped_dev(1, step, wp_mx1, factors[1, step])
+                add_blank(1, step, w1_mx1)
             if step >= 2:
                 quantise_y(step - 2)
+            if step < pairs:
+                quantise_h(1, step)
+            if 1 <= step <= pairs:
+                weigh(step - 1)
         for quad in range(4):
             queue = nc.sync if quad % 2 == 0 else nc.scalar
             queue.dma_start(

from contextlib import ExitStack

import concourse.mybir as mybir

K, K2, H, N, T, S = 1024, 512, 1024, 512, 4096, 1024
FLOPS = 2 * S * (K * H + 2 * K2 * H + H * N)

F32 = mybir.dt.float32
BF16 = mybir.dt.bfloat16
I32 = mybir.dt.int32
U32 = mybir.dt.uint32
U16 = mybir.dt.uint16
U8 = mybir.dt.uint8
FP8X4 = mybir.dt.float8_e4m3fn_x4
FP4X4 = mybir.dt.float4_e2m1fn_x4
ACT = mybir.ActivationFunctionType
ALU = mybir.AluOpType

P = 128
PACK = 4
PASS = P * PACK
COLS = 128
CHUNKS = S // COLS
PAIR = 2 * COLS


def tile_list_lens_path_correction_kernel(
    tc, tab_words, tab_scales, offs, xs_words, xs_scales, w1, wp,
    wq_words, wq_scales, w4_words, w4_scales, place, out_0, out_1, out_2,
):
    nc = tc.nc
    with ExitStack() as ctx:
        keep = ctx.enter_context(tc.tile_pool(name="keep", bufs=1))
        ring = ctx.enter_context(tc.tile_pool(name="ring", bufs=3))
        psum = ctx.enter_context(tc.psum_pool(name="psum", bufs=1))

        def held(shape, dtype, name, over=None):
            return keep.tile(shape, dtype, name=name, tag=over or name, align_bytes=64)

        def load_words(tile, words):
            nc.sync.dma_start(out=tile[:].bitcast(I32), in_=words.bitcast(I32))

        def load_scale_rows(queue, tile, scales):
            passes = scales.shape[0]
            for quad in range(4):
                rows = scales[:, 4 * quad : 4 * quad + 4, :].bitcast(I32)
                queue.dma_start(out=tile[32 * quad : 32 * quad + 4 * passes, :].bitcast(I32), in_=rows)

        offsets = keep.tile([P, S // 16], U16, name="offsets")
        wq_raw = held([P, H], U16, "wq_raw")
        wq_raw_scales = held([P, H], U8, "wq_raw_scales")
        xs_codes = held([P, S], U32, "xs_codes")
        xs_plane = held([P, S], U8, "xs_plane")
        tab_plane = held([P, T], U8, "tab_plane")
        w4_raw_scales = held([P, N], U8, "w4_raw_scales")
        tab_codes = [held([P, T], U32, f"tab_codes{a}") for a in range(2)]
        w4_raw = held([P, 2, N], I32, "w4_raw")
        place_sb = [held([P, PACK, S // 2], F32, f"place{half}") for half in range(2)]

        for plane in (wq_raw_scales, xs_plane):
            nc.gpsimd.memset(plane[:].bitcast(I32), 0)
        for plane in (tab_plane, w4_raw_scales):
            nc.vector.memset(plane[:].bitcast(I32), 0)

        def load_weight(w, a, b, name):
            raw = held([P, PACK, PASS], F32, name)
            rows = w[a * PASS : (a + 1) * PASS, b * PASS : (b + 1) * PASS]
            nc.sync.dma_start(out=raw[:], in_=rows.rearrange("(p i) c -> p i c", i=PACK))
            return raw

        load_words(xs_codes, xs_words[0].rearrange("p c i -> p (c i)"))
        load_words(wq_raw, wq_words[0])
        load_scale_rows(nc.sync, wq_raw_scales, wq_scales)
        load_scale_rows(nc.sync, xs_plane, xs_scales)
        load_scale_rows(nc.sync, tab_plane, tab_scales)
        nc.sync.dma_start(offsets[:], offs)
        wp_raw = [load_weight(wp, 0, 0, "wp_raw0")]
        w1_raw = {(0, 0): load_weight(w1, 0, 0, "w1_raw00")}
        load_words(tab_codes[0], tab_words[0].rearrange("p c i -> p (c i)"))
        w1_raw[1, 0] = load_weight(w1, 1, 0, "w1_raw10")
        load_scale_rows(nc.sync, w4_raw_scales, w4_scales)
        load_words(tab_codes[1], tab_words[1].rearrange("p c i -> p (c i)"))
        wp_raw.append(load_weight(wp, 0, 1, "wp_raw1"))
        for a in range(2):
            w1_raw[a, 1] = load_weight(w1, a, 1, f"w1_raw{a}1")
        nc.sync.dma_start(out=w4_raw[:], in_=w4_words.rearrange("a p c i -> p a (c i)").bitcast(I32))
        for half in range(2):
            cols = slice(half * S // 2, (half + 1) * S // 2)
            nc.sync.dma_start(out=place_sb[half][:], in_=place[:, cols].rearrange("(p t) j -> p t j", t=PACK))

        wq_codes = held([P, H], U16, "wq_codes")
        wq_plane = held([P, H], U8, "wq_plane")
        for b in range(2):
            cols = slice(b * PASS, (b + 1) * PASS)
            for dealt, natural in ((wq_codes, wq_raw), (wq_plane, wq_raw_scales)):
                nc.vector.tensor_copy(
                    out=dealt[:, cols].rearrange("p (t m) -> p t m", t=PACK),
                    in_=natural[:, cols].rearrange("p (m t) -> p t m", t=PACK),
                )

        def round_weight(engine, raw, name, over=None):
            rounded = held([P, PASS * PACK], BF16, name, over)
            dst = rounded[:].rearrange("p (t m i) -> p m i t", t=PACK, i=PACK)
            src = raw[:].rearrange("p i (m t) -> p m i t", t=PACK)
            if engine is nc.vector:
                nc.vector.tensor_copy(out=dst, in_=src)
            else:
                nc.scalar.copy(out=dst, in_=src)
            return rounded

        def quantise(rounded, name, over=None):
            width = rounded.shape[1] // PACK
            codes = held([P, width], U32, name + "_codes", over)
            plane = held([P, width], U8, name + "_plane")
            nc.vector.quantize_mx(out=codes[:].bitcast(FP8X4), scales=plane[:], in_=rounded[:])
            return codes, plane

        def product(bank_number, passes, slices, cols):
            width = cols.stop - cols.start
            bank = psum.tile([P, len(slices), width], F32, name=f"bank{bank_number}")
            for place_in_bank, t in enumerate(slices):
                rows = slice(t * P, (t + 1) * P)
                for n, (w_codes, w_plane, x_codes, x_plane, w_dtype) in enumerate(passes):
                    nc.tensor.matmul_mx(
                        out=bank[:, place_in_bank, :],
                        lhsT=w_codes[:, rows].bitcast(w_dtype),
                        lhsT_scale=w_plane[:, rows],
                        rhs=x_codes[:, cols].bitcast(FP8X4),
                        rhs_scale=x_plane[:, cols],
                        start=(n == 0),
                        stop=(n == len(passes) - 1),
                    )
            return bank

        def chunk_cols(chunk):
            return slice(chunk * COLS, (chunk + 1) * COLS)

        taken = []

        def next_banks():
            first_bank = 2 * len(taken) % 8
            taken.append(first_bank)
            return first_bank

        def woven(bank):
            return bank[:].rearrange("p t c -> p c t")

        def as_woven(ap):
            return ap.rearrange("p (c t) -> p c t", t=PACK)

        factors = {}
        terms = {}

        def square_rough(b, pair):
            cols = slice(b * PASS, (b + 1) * PASS)
            passes = [(wq_codes[:, cols], wq_plane[:, cols], xs_codes[:], xs_plane[:], FP4X4)]
            factor = held([P, 2 * PASS], F32, f"factor{b}_{pair}")
            first_bank = next_banks()
            for half in range(2):
                bank = product(first_bank + half, passes, range(PACK), chunk_cols(2 * pair + half))
                nc.scalar.activation(out=as_woven(factor[:, half * PASS : (half + 1) * PASS]), in_=woven(bank), func=ACT.Square)
            factors[b, pair] = factor

        def damping(b, pair, roots):
            root = roots[:, pair % 2, :]
            nc.scalar.activation(out=root, in_=factors[b, pair][:], func=ACT.Abs_reciprocal_sqrt, bias=1.0)
            nc.scalar.activation(out=factors[b, pair][:], in_=root, func=ACT.Square)

        def damped_dev(b, pair, wp_mx, term):
            first_bank = next_banks()
            for half in range(2):
                passes = [(wp_mx[0][:], wp_mx[1][:], xs_codes[:], xs_plane[:], FP8X4)]
                bank = product(first_bank + half, passes, range(PACK), chunk_cols(2 * pair + half))
                cols = slice(half * PASS, (half + 1) * PASS)
                nc.vector.tensor_tensor(
                    out=as_woven(term[:, cols]), in0=woven(bank), in1=as_woven(factors[b, pair][:, cols]), op=ALU.mult
                )
            terms[b, pair] = term

        v_codes = []
        v_plane = held([P, S], U8, "v_plane")

        h_rounds = {}

        def add_blank(b, pair, w1_mx):
            passes = [(w1_mx[a][0][:], w1_mx[a][1][:], v_codes[a][:], v_plane[4 * a :, :], FP8X4) for a in range(2)]
            h_round = ring.tile([P, 2 * PASS], BF16, name="h_round", align_bytes=64)
            first_bank = next_banks()
            for half in range(2):
                bank = product(first_bank + half, passes, range(PACK), chunk_cols(2 * pair + half))
                cols = slice(half * PASS, (half + 1) * PASS)
                nc.vector.tensor_tensor(
                    out=as_woven(h_round[:, cols]), in0=woven(bank), in1=as_woven(terms[b, pair][:, cols]), op=ALU.add
                )
            h_rounds[b, pair] = h_round

        h_codes = [held([P, S], U32, f"h_codes{b}") for b in range(2)]
        h_plane = [held([P, S], U8, f"h_plane{b}") for b in range(2)]

        def quantise_h(b, pair):
            cols = slice(pair * PAIR, (pair + 1) * PAIR)
            nc.vector.quantize_mx(out=h_codes[b][:, cols].bitcast(FP8X4), scales=h_plane[b][:, cols], in_=h_rounds[b, pair][:])

        pairs = CHUNKS // 2
        for b in range(2):
            for pair in range(pairs):
                square_rough(b, pair)
        roots = held([P, 2, 2 * PASS], F32, "roots0")
        for pair in range(pairs):
            damping(0, pair, roots)

        def gather_words(a, pieces):
            v_codes.append(held([P, S], U32, f"v_codes{a}"))
            width = S // pieces
            for first in range(0, S, width):
                picks = offsets[:, first // 16 : (first + width) // 16]
                nc.vector.tensor_copy(v_codes[a][:, first : first + width], tab_codes[a][:].indirect(picks))

        nc.vector.tensor_copy(v_plane[:], tab_plane[:].indirect(offsets[:]))
        wp_round0 = round_weight(nc.vector, wp_raw[0], "wp_round0")
        w1_round00 = round_weight(nc.vector, w1_raw[0, 0], "w1_round00")
        wp_mx0 = quantise(wp_round0, "wp0")
        w1_mx0 = [quantise(w1_round00, "w1_00")]
        gather_words(0, 1)
        w1_round10 = round_weight(nc.vector, w1_raw[1, 0], "w1_round10")
        w4_plane = held([P, N], U8, "w4_plane")
        nc.vector.tensor_copy(
            out=w4_plane[:].rearrange("p (t m) -> p t m", t=PACK),
            in_=w4_raw_scales[:].rearrange("p (m t) -> p t m", t=PACK),
        )
        w1_mx0.append(quantise(w1_round10, "w1_10"))
        early_terms = held([P, 2, 2 * PASS], F32, "early_terms", "w1_raw10")
        for pair in range(2):
            damped_dev(0, pair, wp_mx0, early_terms[:, pair, :])
        gather_words(1, 2)
        late_terms = held([P, 2, 2 * PASS], F32, "late_terms", "tab_codes1")
        wp_round1 = round_weight(nc.scalar, wp_raw[1], "wp_round1", "roots0")
        w1_round01 = round_weight(nc.scalar, w1_raw[0, 1], "w1_round01", "wp_raw1")
        w1_round11 = round_weight(nc.scalar, w1_raw[1, 1], "w1_round11", "w1_raw01")
        roots = held([P, 2, 2 * PASS], F32, "roots1", "w1_raw11")
        damping(1, 0, roots)

        for pair in range(pairs):
            if 1 <= pair < pairs - 1:
                damped_dev(0, pair + 1, wp_mx0, late_terms[:, pair - 1, :])
            add_blank(0, pair, w1_mx0)
            if pair >= 1:
                quantise_h(0, pair - 1)
        wp_mx1 = quantise(wp_round1, "wp1")
        quantise_h(0, pairs - 1)
        w1_mx1 = [quantise(w1_round01, "w1_01")]
        w4_codes = held([P, 2, N], I32, "w4_codes", "tab_codes1")
        nc.vector.tensor_copy(
            out=w4_codes[:].rearrange("p a (t g m) -> p a g t m", t=PACK, m=4),
            in_=w4_raw[:].rearrange("p a (g m t) -> p a g t m", t=PACK, m=4),
        )
        w1_mx1.append(quantise(w1_round11, "w1_11"))

        y_codes = held([P, S], U32, "y_codes")
        y_plane = held([P, S], U8, "y_plane")
        y_sb = [held([P, PACK, PAIR], F32, f"y{pair}", f"factor0_{pair}") for pair in range(CHUNKS // 2)]
        y_rounds = {}

        def weigh(pair):
            passes = [(w4_codes[:, a, :], w4_plane[4 * a :, :], h_codes[a][:], h_plane[a][:], FP8X4) for a in range(2)]
            y_round = ring.tile([P, PAIR * PACK], BF16, name="y_round", align_bytes=64)
            first_bank = next_banks()
            for half in range(2):
                chunk = 2 * pair + half
                bank = product(first_bank + half, passes, range(PACK), chunk_cols(chunk))
                first = chunk * COLS % (S // 2)
                y = y_sb[pair][:, :, chunk_cols(half)]
                nc.vector.tensor_tensor(
                    out=y, in0=bank[:], in1=place_sb[pair // 2][:, :, first : first + COLS], op=ALU.mult
                )
                dst = y_round[:, half * PASS : (half + 1) * PASS].rearrange("p (g c t) -> p g t c", t=PACK, c=4)
                src = y.rearrange("p t (g c) -> p g t c", c=4)
                if chunk == CHUNKS - 1:
                    nc.vector.tensor_copy(out=dst, in_=src)
                else:
                    nc.scalar.copy(out=dst, in_=src)
            cols = slice(pair * PAIR, (pair + 1) * PAIR)
            nc.sync.dma_start(out=out_0[:, cols].rearrange("(p t) j -> p t j", t=PACK), in_=y_sb[pair][:])
            y_rounds[pair] = y_round

        def quantise_y(pair):
            cols = slice(pair * PAIR, (pair + 1) * PAIR)
            nc.vector.quantize_mx(out=y_codes[:, cols].bitcast(FP8X4), scales=y_plane[:, cols], in_=y_rounds[pair][:])
            nc.sync.dma_start(
                out=out_1[0].rearrange("p c i -> p (c i)").bitcast(I32)[:, cols],
                in_=y_codes[:, cols].bitcast(I32),
            )

        for step in range(pairs + 2):
            if step + 1 < pairs:
                damping(1, step + 1, roots)
            if step < pairs:
                damped_dev(1, step, wp_mx1, factors[1, step])
                add_blank(1, step, w1_mx1)
            if step >= 2:
                quantise_y(step - 2)
            if step < pairs:
                quantise_h(1, step)
            if 1 <= step <= pairs:
                weigh(step - 1)
        for quad in range(4):
            queue = nc.sync if quad % 2 == 0 else nc.scalar
            queue.dma_start(
                out=out_2[0, 4 * quad : 4 * quad + 4, :].bitcast(I32),
                in_=y_plane[32 * quad : 32 * quad + 4, :].bitcast(I32),
            )
